import numpy as np
import ml_dtypes


def mxq(x, axis, fmt="e4m3"):
    dtype, down = {"e4m3": (ml_dtypes.float8_e4m3fn, 7), "e5m2": (ml_dtypes.float8_e5m2, 14)}[fmt]
    v = np.moveaxis(np.asarray(x, np.float32).astype(ml_dtypes.bfloat16).astype(np.float64), axis, -1)
    blocks = v.reshape(v.shape[:-1] + (-1, 32))
    amax = np.abs(blocks).max(-1, keepdims=True)
    byte = np.maximum(np.where(amax > 0, np.frexp(amax)[1] - 1 + 127, 0) - down, 1)
    scale = np.exp2(byte - 127.0)
    codes = (blocks / scale).astype(np.float32).astype(dtype).astype(np.float64)
    return np.moveaxis((codes * scale).reshape(v.shape), -1, axis)


WIDE = False


def mx_kscale(k):
    if not WIDE:
        return np.ones(k)
    levels = np.array([10, -10, 5, -5, 0])
    if k % 512:
        return np.exp2(np.random.permutation(np.resize(levels, k // 32))).repeat(32)
    a = np.empty((k // 512, 16))
    for p in range(k // 512):
        a[p, :8] = np.random.permutation(np.resize(levels, 8))
        for g in range(8):
            far = levels[np.abs(levels - a[p, g]) >= 10]
            a[p, g + 8] = far[np.random.randint(len(far))]
    return np.exp2(a.ravel()).repeat(32)


def f64(x):
    return np.asarray(x).astype(np.float64)


def striped(idx):
    return np.tile(idx.reshape(-1, 16).T, (8, 1)).astype(np.uint16)


def unstriped(offs):
    return offs[:16].T.reshape(-1).astype(np.int64)


def striped8(idx):
    return np.concatenate([x.reshape(-1, 16).T for x in idx]).astype(np.uint16)


def runs(offs, k):
    lists = np.stack([offs[16 * r : 16 * r + 16].T.reshape(-1) for r in range(8)]).astype(np.int64)
    return lists[np.arange(k) % 512 // 64]


def pack_weight(w):
    k, n = w.shape
    w = f64(np.asarray(w, np.float32).astype(ml_dtypes.bfloat16)).reshape(k // 32, 32, n)
    amax = np.abs(w).max(1)
    byte = np.clip(np.where(amax > 0, np.frexp(amax)[1] - 1 + 127 - 7, 1), 1, 254)
    scaled = (w * np.exp2(127.0 - byte)[:, None, :]).reshape(k, n).astype(np.float32)
    words = np.ascontiguousarray(scaled.reshape(k // 512, 128, 4, n).transpose(0, 1, 3, 2)).astype(ml_dtypes.float8_e4m3fn).view(np.uint8)
    return words, np.ascontiguousarray(byte.astype(np.uint8).reshape(k // 512, 16, n))


def unpack_weight(words, scales):
    g, p, n, _ = words.shape
    vals = np.ascontiguousarray(words).view(ml_dtypes.float8_e4m3fn).astype(np.float64) * np.repeat(np.exp2(scales.astype(np.float64) - 127.0), 8, axis=1)[..., None]
    return vals.transpose(0, 1, 3, 2).reshape(g * 512, n)


def sigmoid(v):
    return 1.0 / (1.0 + np.exp(-np.maximum(v, -700.0)))

def planes(y):
    n, m = y.shape
    v = y.astype(np.float32).astype(ml_dtypes.bfloat16).astype(np.float64).reshape(n // 32, 32, m)
    top = np.abs(v).max(1)
    byte = np.clip(np.where(top > 0, np.frexp(top)[1] - 1 + 127 - 7, 1), 1, 254)
    codes = (v * np.exp2(127.0 - byte)[:, None, :]).reshape(n, m).astype(np.float32).astype(ml_dtypes.float8_e4m3fn).view(np.uint8)
    words = codes.reshape(n // 512, 128, 4, m).transpose(0, 1, 3, 2)
    return np.ascontiguousarray(words), np.ascontiguousarray(byte.astype(np.uint8).reshape(n // 512, 16, m))


K, T, S, N = 512, 2048, 512, 512


def setup_inputs():
    n = np.random.standard_normal
    s = mx_kscale(K)[:, None]
    packed_xT = pack_weight(n((K, T)) * s)
    return {
        "x_words": packed_xT[0],
        "x_scales": packed_xT[1],
        "w1": (n((K, N)) / np.sqrt(K) / s).astype(np.float32),
        "dg1": np.random.uniform(0.1, 1.0, (N, S)).astype(np.float32),
        "dg2": np.random.uniform(0.1, 1.0, (N, S)).astype(np.float32),
        "offs": striped(np.random.permutation(T)[:S]),
        "p1": striped8(np.stack([np.random.permutation(S) for _ in range(8)])),
        "p2": striped8(np.stack([np.random.permutation(S) for _ in range(8)])),
    }


def reference(x_words, x_scales, w1, dg1, dg2, offs, p1, p2):
    xq = unpack_weight(x_words, x_scales)[:, unstriped(offs)]
    y = mxq(f64(w1), 0, "e4m3").T @ xq
    out_0 = f64(dg1) * (sigmoid(y[np.arange(N)[:, None], runs(p1, N)] - y)) + f64(dg2) * (sigmoid(y[np.arange(N)[:, None], runs(p2, N)] - y))
    return (out_0,) + planes(out_0)

@@ -1,0 +1,177 @@
+from contextlib import ExitStack
+
+import concourse.mybir as mybir
+
+K, T, S, N = 512, 2048, 512, 512
+FLOPS = 2 * K * N * S
+
+F32 = mybir.dt.float32
+BF16 = mybir.dt.bfloat16
+I32 = mybir.dt.int32
+U32 = mybir.dt.uint32
+U16 = mybir.dt.uint16
+U8 = mybir.dt.uint8
+FP8X4 = mybir.dt.float8_e4m3fn_x4
+ALU = mybir.AluOpType
+ACT = mybir.ActivationFunctionType
+
+P = 128
+PACK = 4
+HALF = 256
+CHUNKS = ((0, 256), (256, 384), (384, 512))
+
+
+def tile_picked_lamrank_none_po_kernel(tc, x_words, x_scales, w1, dg1, dg2, offs, p1, p2, out_0, out_1, out_2):
+    nc = tc.nc
+    with ExitStack() as ctx:
+        keep = ctx.enter_context(tc.tile_pool(name="keep", bufs=1))
+        psum = ctx.enter_context(tc.psum_pool(name="psum", bufs=1))
+
+        offs_sb = keep.tile([P, S // 16], U16, name="offs_sb")
+        lists = [keep.tile([P, S // 16], U16, name=f"list{i}") for i in range(2)]
+        xw = keep.tile([P, T], U32, name="xw")
+        xs = keep.tile([P, T], U8, name="xs")
+        w_rows = w1.rearrange("(p j) c -> p j c", j=PACK)
+        w_raw = [keep.tile([P, PACK, HALF], F32, name=f"w_raw{h}", tag=f"stage{h}") for h in range(2)]
+
+        nc.vector.memset(xs[:].bitcast(I32), 0)
+        for q in range(4):
+            queue = nc.sync if q == 0 else nc.scalar
+            queue.dma_start(xs[32 * q : 32 * q + 4, :].bitcast(I32), x_scales[0, 4 * q : 4 * q + 4, :].bitcast(I32))
+        nc.sync.dma_start(offs_sb[:], offs)
+        nc.sync.dma_start(w_raw[0][:], w_rows[:, :, 0:HALF])
+        nc.sync.dma_start(xw[:].bitcast(I32), x_words[0].rearrange("p n t -> p (n t)").bitcast(I32))
+        nc.sync.dma_start(w_raw[1][:], w_rows[:, :, HALF:N])
+        nc.sync.dma_start(lists[0][:], p1)
+        nc.sync.dma_start(lists[1][:], p2)
+
+        w_bf = keep.tile([P, PACK, P, PACK], BF16, name="w_bf", align_bytes=64)
+
+        def cast(eng_copy, h, m0, m1):
+            eng_copy(
+                w_bf[:, :, 64 * h + m0 : 64 * h + m1, :].rearrange("p t m j -> p m t j"),
+                w_raw[h][:].rearrange("p j (m t) -> p m t j", t=PACK)[:, m0:m1, :, :],
+            )
+
+        cast(nc.scalar.copy, 0, 0, 64)
+        xs_g = keep.tile([P, S], U8, name="xs_g", align_bytes=64)
+        nc.vector.tensor_copy(xs_g[:], xs[:].indirect(offs_sb[:]))
+        xw_g = [keep.tile([P, HALF], U32, name=f"xw_g{h}", align_bytes=64) for h in range(2)]
+        for h in range(2):
+            nc.vector.tensor_copy(xw_g[h][:], xw[:].indirect(offs_sb[:, 16 * h : 16 * h + 16]))
+        cast(nc.scalar.copy, 1, 0, 20)
+        cast(nc.vector.tensor_copy, 1, 20, 64)
+        w_codes = [keep.tile([P, P], U32, name=f"w_codes{t}", align_bytes=64) for t in range(PACK)]
+        w_scales = [keep.tile([P, P], U8, name=f"w_scales{t}", align_bytes=64) for t in range(PACK)]
+        for t in range(PACK):
+            nc.vector.quantize_mx(w_codes[t][:].bitcast(FP8X4), w_scales[t][:], w_bf[:, t, :, :].rearrange("p m j -> p (m j)"))
+
+        gains = []
+        for h in range(2):
+            g = keep.tile([P, PACK, 2, HALF], F32, name=f"gain{h}", tag=f"stage{h}")
+            for i, dg in enumerate((dg1, dg2)):
+                nc.sync.dma_start(g[:, :, i, :], dg.rearrange("(p t) s -> p t s", t=PACK)[:, :, HALF * h : HALF * h + HALF])
+            gains.append(g)
+
+        win = [keep.tile([P, S], F32, name=f"win{t}") for t in range(PACK)]
+        plain = [[keep.tile([P, HALF], F32, name=f"plain{t}_{h}") for h in range(2)] for t in range(PACK)]
+        banks = {}
+        for t in range(PACK):
+            for h in range(2):
+                bank = psum.tile([P, HALF], F32, name=f"bank{t}_{h}")
+                nc.tensor.matmul_mx(
+                    bank[:],
+                    lhsT=w_codes[t][:].bitcast(FP8X4),
+                    lhsT_scale=w_scales[t][:],
+                    rhs=xw_g[h][:].bitcast(FP8X4),
+                    rhs_scale=xs_g[:, HALF * h : HALF * h + HALF],
+                    start=True,
+                    stop=True,
+                )
+                banks[t, h] = bank
+
+        def empty(t):
+            nc.scalar.copy(win[t][:, 0:HALF], banks[t, 0][:])
+            nc.scalar.copy(plain[t][0][:], banks[t, 0][:])
+            if t == 0:
+                nc.vector.tensor_copy(win[t][:, HALF:S], banks[t, 1][:])
+            else:
+                nc.scalar.copy(win[t][:, HALF:S], banks[t, 1][:])
+
+        o_scales = keep.tile([P, S], U8, name="o_scales", align_bytes=64)
+        out_rows = out_0.rearrange("(p t) s -> p t s", t=PACK)
+        words_hbm = out_1[0].rearrange("p n t -> p (n t)").bitcast(I32)
+        res = [keep.tile([P, PACK, c1 - c0], F32, name=f"res{c}") for c, (c0, c1) in enumerate(CHUNKS)]
+        units = [(c, t) for c in range(len(CHUNKS)) for t in range(PACK)]
+        diff, sig, prod = {}, {}, {}
+
+        def gather(u, i):
+            c, t = units[u]
+            c0, c1 = CHUNKS[c]
+            if i == 0:
+                diff[u] = keep.tile([P, 2, c1 - c0], F32, name=f"diff{u}")
+            h = c0 // HALF
+            nc.vector.tensor_tensor(
+                diff[u][:, i, :],
+                win[t][:].indirect(lists[i][:, c0 // 16 : c1 // 16]),
+                plain[t][h][:, c0 - HALF * h : c1 - HALF * h],
+                ALU.subtract,
+            )
+
+        def sigmoid(u):
+            c, t = units[u]
+            c0, c1 = CHUNKS[c]
+            sig[u] = keep.tile([P, 2, c1 - c0], F32, name=f"sig{u}")
+            nc.scalar.activation(sig[u][:], diff[u][:], ACT.Sigmoid)
+
+        def weigh(u):
+            c, t = units[u]
+            c0, c1 = CHUNKS[c]
+            prod[u] = keep.tile([P, 2, c1 - c0], F32, name=f"prod{u}")
+            nc.vector.tensor_tensor(prod[u][:], sig[u][:], gains[c0 // HALF][:, t, :, c0 % HALF : c0 % HALF + c1 - c0], ALU.mult)
+
+        def total(u):
+            c, t = units[u]
+            nc.vector.tensor_tensor(res[c][:, t, :], prod[u][:, 0, :], prod[u][:, 1, :], ALU.add)
+
+        rounded = {}
+
+        def round_chunk(c):
+            c0, c1 = CHUNKS[c]
+            nc.sync.dma_start(out_rows[:, :, c0:c1], res[c][:])
+            rounded[c] = keep.tile([P, c1 - c0, PACK], BF16, name=f"rounded{c}", align_bytes=64)
+            nc.scalar.copy(
+                rounded[c][:].rearrange("p (a i) t -> p a t i", i=4),
+                res[c][:].rearrange("p t (a i) -> p a t i", i=4),
+            )
+
+        def quantise_chunk(c):
+            c0, c1 = CHUNKS[c]
+            codes = keep.tile([P, c1 - c0], U32, name=f"codes{c}", align_bytes=64)
+            nc.vector.quantize_mx(codes[:].bitcast(FP8X4), o_scales[:, c0:c1], rounded[c][:].rearrange("p n t -> p (n t)"))
+            nc.sync.dma_start(words_hbm[:, c0:c1], codes[:].bitcast(I32))
+
+        empty(0)
+        last = len(units) - 1
+        for u in range(len(units) + 1):
+            if u + 1 < PACK:
+                empty(u + 1)
+            if PACK - 1 <= u < 2 * PACK - 1:
+                nc.scalar.copy(plain[u - PACK + 1][1][:], banks[u - PACK + 1, 1][:])
+            if u <= last:
+                gather(u, 0)
+            if u >= 1:
+                weigh(u - 1)
+            if u <= last:
+                gather(u, 1)
+                sigmoid(u)
+            if u >= 1:
+                total(u - 1)
+                if (u - 1) % PACK == PACK - 1:
+                    round_chunk((u - 1) // PACK)
+            if u >= 2 and (u - 2) % PACK == PACK - 1:
+                quantise_chunk((u - 2) // PACK)
+        quantise_chunk(len(CHUNKS) - 1)
+        for q in range(4):
+            eng = nc.sync if q % 2 == 0 else nc.scalar
+            eng.dma_start(out_2[0, 4 * q : 4 * q + 4, :].bitcast(I32), o_scales[32 * q : 32 * q + 4, :].bitcast(I32))

@@ -19,6 +19,7 @@ P = 128
 PACK = 4
 HALF = 256
 CHUNKS = ((0, 256), (256, 384), (384, 512))
+GROUPS = (((0, 1), (1, 2), (2, 4)), ((0, 4),), ((0, 3), (3, 4)))
 
 
 def tile_picked_lamrank_none_po_kernel(tc, x_words, x_scales, w1, dg1, dg2, offs, p1, p2, out_0, out_1, out_2):
@@ -30,120 +31,114 @@ def tile_picked_lamrank_none_po_kernel(tc, x_words, x_scales, w1, dg1, dg2, offs
         offs_sb = keep.tile([P, S // 16], U16, name="offs_sb")
         lists = [keep.tile([P, S // 16], U16, name=f"list{i}") for i in range(2)]
         xw = keep.tile([P, T], U32, name="xw")
-        xs = keep.tile([P, T], U8, name="xs")
-        w_rows = w1.rearrange("(p j) c -> p j c", j=PACK)
-        w_raw = [keep.tile([P, PACK, HALF], F32, name=f"w_raw{h}", tag=f"stage{h}") for h in range(2)]
+        xs = keep.tile([P, T], U8, name="xs", tag="w_codes0", align_bytes=64)
+        w_raw = keep.tile([P, PACK * N], F32, name="w_raw", tag="stage")
 
         nc.vector.memset(xs[:].bitcast(I32), 0)
-        for q in range(4):
-            queue = nc.sync if q == 0 else nc.scalar
-            queue.dma_start(xs[32 * q : 32 * q + 4, :].bitcast(I32), x_scales[0, 4 * q : 4 * q + 4, :].bitcast(I32))
         nc.sync.dma_start(offs_sb[:], offs)
-        nc.sync.dma_start(w_raw[0][:], w_rows[:, :, 0:HALF])
+        for q in range(4):
+            nc.scalar.dma_start(xs[32 * q : 32 * q + 4, :].bitcast(I32), x_scales[0, 4 * q : 4 * q + 4, :].bitcast(I32))
+        nc.sync.dma_start(w_raw[:], w1.rearrange("(p j) c -> p (j c)", j=PACK))
         nc.sync.dma_start(xw[:].bitcast(I32), x_words[0].rearrange("p n t -> p (n t)").bitcast(I32))
-        nc.sync.dma_start(w_raw[1][:], w_rows[:, :, HALF:N])
         nc.sync.dma_start(lists[0][:], p1)
         nc.sync.dma_start(lists[1][:], p2)
+        warm = keep.tile([P, 2], F32, name="warm")
+        nc.vector.memset(warm[:, 0:1], 0.0)
+        nc.scalar.activation(warm[:, 1:2], warm[:, 0:1], ACT.Sigmoid)
 
-        w_bf = keep.tile([P, PACK, P, PACK], BF16, name="w_bf", align_bytes=64)
-
-        def cast(eng_copy, h, m0, m1):
-            eng_copy(
-                w_bf[:, :, 64 * h + m0 : 64 * h + m1, :].rearrange("p t m j -> p m t j"),
-                w_raw[h][:].rearrange("p j (m t) -> p m t j", t=PACK)[:, m0:m1, :, :],
-            )
-
-        cast(nc.scalar.copy, 0, 0, 64)
         xs_g = keep.tile([P, S], U8, name="xs_g", align_bytes=64)
         nc.vector.tensor_copy(xs_g[:], xs[:].indirect(offs_sb[:]))
-        xw_g = [keep.tile([P, HALF], U32, name=f"xw_g{h}", align_bytes=64) for h in range(2)]
-        for h in range(2):
-            nc.vector.tensor_copy(xw_g[h][:], xw[:].indirect(offs_sb[:, 16 * h : 16 * h + 16]))
-        cast(nc.scalar.copy, 1, 0, 20)
-        cast(nc.vector.tensor_copy, 1, 20, 64)
-        w_codes = [keep.tile([P, P], U32, name=f"w_codes{t}", align_bytes=64) for t in range(PACK)]
-        w_scales = [keep.tile([P, P], U8, name=f"w_scales{t}", align_bytes=64) for t in range(PACK)]
-        for t in range(PACK):
-            nc.vector.quantize_mx(w_codes[t][:].bitcast(FP8X4), w_scales[t][:], w_bf[:, t, :, :].rearrange("p m j -> p (m j)"))
 
-        gains = []
+        w_src = w_raw[:].rearrange("p (j m t) -> p m t j", j=PACK, t=PACK)
+        w_codes, w_scales = [], []
+        for pair, copy in enumerate((nc.vector.tensor_copy, nc.scalar.copy)):
+            w_bf = keep.tile([P, 2, P, PACK], BF16, name=f"w_bf{pair}", tag=f"w_bf{pair}", align_bytes=64)
+            copy(w_bf[:].rearrange("p t m j -> p m t j"), w_src[:, :, 2 * pair : 2 * pair + 2, :])
+            codes = keep.tile([P, 2 * P], U32, name=f"w_codes{pair}", tag=f"w_codes{pair}", align_bytes=64)
+            scales = keep.tile([P, 2 * P], U8, name=f"w_scales{pair}", align_bytes=64)
+            nc.vector.quantize_mx(codes[:].bitcast(FP8X4), scales[:], w_bf[:].rearrange("p t m j -> p (t m j)"))
+            w_codes.append(codes)
+            w_scales.append(scales)
+
+        xw_g = keep.tile([P, S], U32, name="xw_g", tag="w_bf0", align_bytes=64)
         for h in range(2):
-            g = keep.tile([P, PACK, 2, HALF], F32, name=f"gain{h}", tag=f"stage{h}")
+            nc.vector.tensor_copy(xw_g[:, HALF * h : HALF * h + HALF], xw[:].indirect(offs_sb[:, 16 * h : 16 * h + 16]))
+
+        gain_all = keep.tile([P, 2 * PACK * S], F32, name="gain_all", tag="stage")
+        gains = []
+        for c0, c1 in CHUNKS:
+            g = gain_all[:, 2 * PACK * c0 : 2 * PACK * c1].rearrange("p (i t n) -> p i t n", t=PACK, i=2)
             for i, dg in enumerate((dg1, dg2)):
-                nc.sync.dma_start(g[:, :, i, :], dg.rearrange("(p t) s -> p t s", t=PACK)[:, :, HALF * h : HALF * h + HALF])
+                nc.sync.dma_start(g[:, i, :, :], dg.rearrange("(p t) s -> p t s", t=PACK)[:, :, c0:c1])
             gains.append(g)
 
         win = [keep.tile([P, S], F32, name=f"win{t}") for t in range(PACK)]
+        banks = [[psum.tile([P, HALF], F32, name=f"bank{t}_{h}") for h in range(2)] for t in range(PACK)]
         plain = [[keep.tile([P, HALF], F32, name=f"plain{t}_{h}") for h in range(2)] for t in range(PACK)]
-        banks = {}
         for t in range(PACK):
             for h in range(2):
-                bank = psum.tile([P, HALF], F32, name=f"bank{t}_{h}")
+                cols = slice(HALF * h, HALF * h + HALF)
                 nc.tensor.matmul_mx(
-                    bank[:],
-                    lhsT=w_codes[t][:].bitcast(FP8X4),
-                    lhsT_scale=w_scales[t][:],
-                    rhs=xw_g[h][:].bitcast(FP8X4),
-                    rhs_scale=xs_g[:, HALF * h : HALF * h + HALF],
+                    banks[t][h][:],
+                    lhsT=w_codes[t // 2][:, P * (t % 2) : P * (t % 2) + P].bitcast(FP8X4),
+                    lhsT_scale=w_scales[t // 2][:, P * (t % 2) : P * (t % 2) + P],
+                    rhs=xw_g[:, cols].bitcast(FP8X4),
+                    rhs_scale=xs_g[:, cols],
                     start=True,
                     stop=True,
                 )
-                banks[t, h] = bank
-
-        def empty(t):
-            nc.scalar.copy(win[t][:, 0:HALF], banks[t, 0][:])
-            nc.scalar.copy(plain[t][0][:], banks[t, 0][:])
-            if t == 0:
-                nc.vector.tensor_copy(win[t][:, HALF:S], banks[t, 1][:])
-            else:
-                nc.scalar.copy(win[t][:, HALF:S], banks[t, 1][:])
+                if (t, h) == (0, 1):
+                    nc.vector.tensor_copy(win[t][:, cols], banks[t][h][:])
+                else:
+                    nc.scalar.copy(win[t][:, cols], banks[t][h][:])
+                if h == 0:
+                    nc.scalar.copy(plain[t][0][:], banks[t][0][:])
 
         o_scales = keep.tile([P, S], U8, name="o_scales", align_bytes=64)
         out_rows = out_0.rearrange("(p t) s -> p t s", t=PACK)
         words_hbm = out_1[0].rearrange("p n t -> p (n t)").bitcast(I32)
         res = [keep.tile([P, PACK, c1 - c0], F32, name=f"res{c}") for c, (c0, c1) in enumerate(CHUNKS)]
-        units = [(c, t) for c in range(len(CHUNKS)) for t in range(PACK)]
-        diff, sig, prod = {}, {}, {}
+        groups = [(c, t0, t1) for c in range(len(CHUNKS)) for t0, t1 in GROUPS[c]]
+        picked, sig, prod, rounded = {}, {}, {}, {}
 
-        def gather(u, i):
-            c, t = units[u]
+        def gather(g, t, i):
+            c, t0, t1 = groups[g]
             c0, c1 = CHUNKS[c]
-            if i == 0:
-                diff[u] = keep.tile([P, 2, c1 - c0], F32, name=f"diff{u}")
             h = c0 // HALF
-            nc.vector.tensor_tensor(
-                diff[u][:, i, :],
-                win[t][:].indirect(lists[i][:, c0 // 16 : c1 // 16]),
-                plain[t][h][:, c0 - HALF * h : c1 - HALF * h],
-                ALU.subtract,
-            )
+            if (t, i) == (t0, 0):
+                picked[g] = keep.tile([P, 2, t1 - t0, c1 - c0], F32, name=f"picked{g}")
+            window = win[t][:].indirect(lists[i][:, c0 // 16 : c1 // 16])
+            own = plain[t][h][:, c0 - HALF * h : c1 - HALF * h]
+            nc.vector.tensor_tensor(picked[g][:, i, t - t0, :], window, own, ALU.subtract)
 
-        def sigmoid(u):
-            c, t = units[u]
+        def sigmoid(g):
+            c, t0, t1 = groups[g]
             c0, c1 = CHUNKS[c]
-            sig[u] = keep.tile([P, 2, c1 - c0], F32, name=f"sig{u}")
-            nc.scalar.activation(sig[u][:], diff[u][:], ACT.Sigmoid)
+            h = c0 // HALF
+            diff = picked[g]
+            sig[g] = keep.tile([P, 2, t1 - t0, c1 - c0], F32, name=f"sig{g}")
+            nc.scalar.activation(sig[g][:], diff[:], ACT.Sigmoid)
+            if c == 0:
+                for t in range(t0, t1):
+                    nc.scalar.copy(plain[t][1][:], banks[t][1][:])
 
-        def weigh(u):
-            c, t = units[u]
+        def weigh(eng, g):
+            c, t0, t1 = groups[g]
             c0, c1 = CHUNKS[c]
-            prod[u] = keep.tile([P, 2, c1 - c0], F32, name=f"prod{u}")
-            nc.vector.tensor_tensor(prod[u][:], sig[u][:], gains[c0 // HALF][:, t, :, c0 % HALF : c0 % HALF + c1 - c0], ALU.mult)
+            prod[g] = keep.tile([P, 2, t1 - t0, c1 - c0], F32, name=f"prod{g}")
+            eng.tensor_tensor(prod[g][:], sig[g][:], gains[c][:, :, t0:t1, :], ALU.mult)
 
-        def total(u):
-            c, t = units[u]
-            nc.vector.tensor_tensor(res[c][:, t, :], prod[u][:, 0, :], prod[u][:, 1, :], ALU.add)
-
-        rounded = {}
-
-        def round_chunk(c):
-            c0, c1 = CHUNKS[c]
-            nc.sync.dma_start(out_rows[:, :, c0:c1], res[c][:])
-            rounded[c] = keep.tile([P, c1 - c0, PACK], BF16, name=f"rounded{c}", align_bytes=64)
-            nc.scalar.copy(
-                rounded[c][:].rearrange("p (a i) t -> p a t i", i=4),
-                res[c][:].rearrange("p t (a i) -> p a t i", i=4),
-            )
+        def total(eng, g):
+            c, t0, t1 = groups[g]
+            eng.tensor_tensor(res[c][:, t0:t1, :], prod[g][:, 0, :, :], prod[g][:, 1, :, :], ALU.add)
+            if t1 == PACK:
+                c0, c1 = CHUNKS[c]
+                nc.sync.dma_start(out_rows[:, :, c0:c1], res[c][:])
+                rounded[c] = keep.tile([P, c1 - c0, PACK], BF16, name=f"rounded{c}", align_bytes=64)
+                nc.scalar.copy(
+                    rounded[c][:].rearrange("p (a i) t -> p a t i", i=4),
+                    res[c][:].rearrange("p t (a i) -> p a t i", i=4),
+                )
 
         def quantise_chunk(c):
             c0, c1 = CHUNKS[c]
@@ -151,27 +146,22 @@ def tile_picked_lamrank_none_po_kernel(tc, x_words, x_scales, w1, dg1, dg2, offs
             nc.vector.quantize_mx(codes[:].bitcast(FP8X4), o_scales[:, c0:c1], rounded[c][:].rearrange("p n t -> p (n t)"))
             nc.sync.dma_start(words_hbm[:, c0:c1], codes[:].bitcast(I32))
 
-        empty(0)
-        last = len(units) - 1
-        for u in range(len(units) + 1):
-            if u + 1 < PACK:
-                empty(u + 1)
-            if PACK - 1 <= u < 2 * PACK - 1:
-                nc.scalar.copy(plain[u - PACK + 1][1][:], banks[u - PACK + 1, 1][:])
-            if u <= last:
-                gather(u, 0)
-            if u >= 1:
-                weigh(u - 1)
-            if u <= last:
-                gather(u, 1)
-                sigmoid(u)
-            if u >= 1:
-                total(u - 1)
-                if (u - 1) % PACK == PACK - 1:
-                    round_chunk((u - 1) // PACK)
-            if u >= 2 and (u - 2) % PACK == PACK - 1:
-                quantise_chunk((u - 2) // PACK)
+        for g in range(len(groups) + 1):
+            steps = [(t, i) for t in range(groups[g][1], groups[g][2]) for i in range(2)] if g < len(groups) else []
+            for k, (t, i) in enumerate(steps):
+                gather(g, t, i)
+                if g >= 1 and k == 0:
+                    weigh(nc.vector, g - 1)
+                if g >= 1 and k == 1:
+                    total(nc.vector, g - 1)
+            if steps:
+                sigmoid(g)
+            else:
+                weigh(nc.vector, g - 1)
+                total(nc.vector, g - 1)
+            if g >= 2 and groups[g - 2][2] == PACK:
+                quantise_chunk(groups[g - 2][0])
         quantise_chunk(len(CHUNKS) - 1)
         for q in range(4):
-            eng = nc.sync if q % 2 == 0 else nc.scalar
-            eng.dma_start(out_2[0, 4 * q : 4 * q + 4, :].bitcast(I32), o_scales[32 * q : 32 * q + 4, :].bitcast(I32))
+            queue = nc.sync if q % 2 == 0 else nc.scalar
+            queue.dma_start(out_2[0, 4 * q : 4 * q + 4, :].bitcast(I32), o_scales[32 * q : 32 * q + 4, :].bitcast(I32))

@@ -1,6 +1,7 @@
 from contextlib import ExitStack
 
 import concourse.mybir as mybir
+from concourse.masks import make_identity
 
 K, T, S, N = 512, 2048, 512, 512
 FLOPS = 2 * K * N * S
@@ -20,6 +21,7 @@ PACK = 4
 HALF = 256
 CHUNKS = ((0, 256), (256, 384), (384, 512))
 GROUPS = (((0, 1), (1, 2), (2, 4)), ((0, 4),), ((0, 3), (3, 4)))
+TENSOR_CHUNKS = 1
 
 
 def tile_picked_lamrank_none_po_kernel(tc, x_words, x_scales, w1, dg1, dg2, offs, p1, p2, out_0, out_1, out_2):
@@ -31,13 +33,15 @@ def tile_picked_lamrank_none_po_kernel(tc, x_words, x_scales, w1, dg1, dg2, offs
         offs_sb = keep.tile([P, S // 16], U16, name="offs_sb")
         lists = [keep.tile([P, S // 16], U16, name=f"list{i}") for i in range(2)]
         xw = keep.tile([P, T], U32, name="xw")
-        xs = keep.tile([P, T], U8, name="xs", tag="w_codes0", align_bytes=64)
+        xs_rows = keep.tile([P, T // 4], I32, name="xs_rows")
+        xs = keep.tile([P, T // 4], I32, name="xs")
         w_raw = keep.tile([P, PACK * N], F32, name="w_raw", tag="stage")
 
-        nc.vector.memset(xs[:].bitcast(I32), 0)
-        nc.sync.dma_start(offs_sb[:], offs)
+        nc.vector.memset(xs[:], 0)
         for q in range(4):
-            nc.scalar.dma_start(xs[32 * q : 32 * q + 4, :].bitcast(I32), x_scales[0, 4 * q : 4 * q + 4, :].bitcast(I32))
+            queue = nc.sync if q % 2 == 0 else nc.scalar
+            queue.dma_start(xs_rows[32 * q : 32 * q + 4, :], x_scales[0, 4 * q : 4 * q + 4, :].bitcast(I32))
+        nc.sync.dma_start(offs_sb[:], offs)
         nc.sync.dma_start(w_raw[:], w1.rearrange("(p j) c -> p (j c)", j=PACK))
         nc.sync.dma_start(xw[:].bitcast(I32), x_words[0].rearrange("p n t -> p (n t)").bitcast(I32))
         nc.sync.dma_start(lists[0][:], p1)
@@ -46,15 +50,19 @@ def tile_picked_lamrank_none_po_kernel(tc, x_words, x_scales, w1, dg1, dg2, offs
         nc.vector.memset(warm[:, 0:1], 0.0)
         nc.scalar.activation(warm[:, 1:2], warm[:, 0:1], ACT.Sigmoid)
 
+        for q in range(4):
+            nc.vector.tensor_copy(xs[32 * q : 32 * q + 4, :], xs_rows[32 * q : 32 * q + 4, :])
+        ident = keep.tile([P, P], F32, name="ident")
+        make_identity(nc, ident[:])
         xs_g = keep.tile([P, S], U8, name="xs_g", align_bytes=64)
-        nc.vector.tensor_copy(xs_g[:], xs[:].indirect(offs_sb[:]))
+        nc.vector.tensor_copy(xs_g[:], xs[:].bitcast(U8).indirect(offs_sb[:]))
 
         w_src = w_raw[:].rearrange("p (j m t) -> p m t j", j=PACK, t=PACK)
         w_codes, w_scales = [], []
         for pair, copy in enumerate((nc.vector.tensor_copy, nc.scalar.copy)):
             w_bf = keep.tile([P, 2, P, PACK], BF16, name=f"w_bf{pair}", tag=f"w_bf{pair}", align_bytes=64)
             copy(w_bf[:].rearrange("p t m j -> p m t j"), w_src[:, :, 2 * pair : 2 * pair + 2, :])
-            codes = keep.tile([P, 2 * P], U32, name=f"w_codes{pair}", tag=f"w_codes{pair}", align_bytes=64)
+            codes = keep.tile([P, 2 * P], U32, name=f"w_codes{pair}", align_bytes=64)
             scales = keep.tile([P, 2 * P], U8, name=f"w_scales{pair}", align_bytes=64)
             nc.vector.quantize_mx(codes[:].bitcast(FP8X4), scales[:], w_bf[:].rearrange("p t m j -> p (t m j)"))
             w_codes.append(codes)
@@ -73,7 +81,7 @@ def tile_picked_lamrank_none_po_kernel(tc, x_words, x_scales, w1, dg1, dg2, offs
             gains.append(g)
 
         win = [keep.tile([P, S], F32, name=f"win{t}") for t in range(PACK)]
-        banks = [[psum.tile([P, HALF], F32, name=f"bank{t}_{h}") for h in range(2)] for t in range(PACK)]
+        banks = [[psum.tile([P, HALF], F32, name=f"bank{t}_{h}", tag=f"bank{t}_{h}") for h in range(2)] for t in range(PACK)]
         plain = [[keep.tile([P, HALF], F32, name=f"plain{t}_{h}") for h in range(2)] for t in range(PACK)]
         for t in range(PACK):
             for h in range(2):
@@ -106,7 +114,7 @@ def tile_picked_lamrank_none_po_kernel(tc, x_words, x_scales, w1, dg1, dg2, offs
             c0, c1 = CHUNKS[c]
             h = c0 // HALF
             if (t, i) == (t0, 0):
-                picked[g] = keep.tile([P, 2, t1 - t0, c1 - c0], F32, name=f"picked{g}")
+                picked[g] = keep.tile([P, 2, t1 - t0, c1 - c0], F32, name=f"picked{g}", tag=f"sig{g - 2}" if g >= 3 else f"picked{g}")
             window = win[t][:].indirect(lists[i][:, c0 // 16 : c1 // 16])
             own = plain[t][h][:, c0 - HALF * h : c1 - HALF * h]
             nc.vector.tensor_tensor(picked[g][:, i, t - t0, :], window, own, ALU.subtract)
@@ -116,7 +124,7 @@ def tile_picked_lamrank_none_po_kernel(tc, x_words, x_scales, w1, dg1, dg2, offs
             c0, c1 = CHUNKS[c]
             h = c0 // HALF
             diff = picked[g]
-            sig[g] = keep.tile([P, 2, t1 - t0, c1 - c0], F32, name=f"sig{g}")
+            sig[g] = keep.tile([P, 2, t1 - t0, c1 - c0], F32, name=f"sig{g}", tag=f"sig{g}")
             nc.scalar.activation(sig[g][:], diff[:], ACT.Sigmoid)
             if c == 0:
                 for t in range(t0, t1):
@@ -128,17 +136,43 @@ def tile_picked_lamrank_none_po_kernel(tc, x_words, x_scales, w1, dg1, dg2, offs
             prod[g] = keep.tile([P, 2, t1 - t0, c1 - c0], F32, name=f"prod{g}")
             eng.tensor_tensor(prod[g][:], sig[g][:], gains[c][:, :, t0:t1, :], ALU.mult)
 
+        turned = {}
+
+        def weave(copy, dst, src):
+            copy(dst.rearrange("p (a i) t -> p a t i", i=4), src.rearrange("p t (a i) -> p a t i", i=4))
+
         def total(eng, g):
             c, t0, t1 = groups[g]
-            eng.tensor_tensor(res[c][:, t0:t1, :], prod[g][:, 0, :, :], prod[g][:, 1, :, :], ALU.add)
-            if t1 == PACK:
-                c0, c1 = CHUNKS[c]
-                nc.sync.dma_start(out_rows[:, :, c0:c1], res[c][:])
-                rounded[c] = keep.tile([P, c1 - c0, PACK], BF16, name=f"rounded{c}", align_bytes=64)
-                nc.scalar.copy(
-                    rounded[c][:].rearrange("p (a i) t -> p a t i", i=4),
-                    res[c][:].rearrange("p t (a i) -> p a t i", i=4),
-                )
+            c0, c1 = CHUNKS[c]
+            on_tensor = c < TENSOR_CHUNKS
+            if on_tensor:
+                for b in range(c0 // P, c1 // P):
+                    if t0 == 0:
+                        turned[b] = psum.tile([P, PACK, P], F32, name=f"turned{b}", tag=f"bank{b}_0")
+                    for t in range(t0, t1):
+                        for i in range(2):
+                            block = prod[g][:, i, t - t0, P * b - c0 : P * b - c0 + P]
+                            nc.tensor.matmul(turned[b][:, t, :], block, ident[:], start=i == 0, stop=i == 1, is_transpose=True)
+            else:
+                eng.tensor_tensor(res[c][:, t0:t1, :], prod[g][:, 0, :, :], prod[g][:, 1, :, :], ALU.add)
+            if t1 < PACK:
+                return
+            rounded[c] = keep.tile([P, c1 - c0, PACK], BF16, name=f"rounded{c}", align_bytes=64)
+            if on_tensor:
+                for b in range(c0 // P, c1 // P):
+                    cols = slice(P * b - c0, P * b - c0 + P)
+                    staged = keep.tile([P, PACK, P], F32, name=f"staged{b}")
+                    nc.scalar.copy(staged[:], turned[b][:])
+                    back = psum.tile([P, PACK, P], F32, name=f"back{b}", tag=f"bank{b}_1")
+                    for t in range(PACK):
+                        nc.tensor.transpose(back[:, t, :], staged[:, t, :], ident[:])
+                    nc.scalar.copy(res[c][:, :, cols], back[:])
+                    weave(nc.scalar.copy, rounded[c][:, cols, :], back[:])
+            else:
+                mid = (c1 - c0) // 2
+                weave(nc.scalar.copy, rounded[c][:, 0:mid, :], res[c][:, :, 0:mid])
+                weave(nc.vector.tensor_copy, rounded[c][:, mid:, :], res[c][:, :, mid:])
+            nc.sync.dma_start(out_rows[:, :, c0:c1], res[c][:])
 
         def quantise_chunk(c):
             c0, c1 = CHUNKS[c]
@@ -159,9 +193,8 @@ def tile_picked_lamrank_none_po_kernel(tc, x_words, x_scales, w1, dg1, dg2, offs
             else:
                 weigh(nc.vector, g - 1)
                 total(nc.vector, g - 1)
-            if g >= 2 and groups[g - 2][2] == PACK:
-                quantise_chunk(groups[g - 2][0])
-        quantise_chunk(len(CHUNKS) - 1)
+        for c in range(len(CHUNKS)):
+            quantise_chunk(c)
         for q in range(4):
             queue = nc.sync if q % 2 == 0 else nc.scalar
             queue.dma_start(out_2[0, 4 * q : 4 * q + 4, :].bitcast(I32), o_scales[32 * q : 32 * q + 4, :].bitcast(I32))

from contextlib import ExitStack

import concourse.mybir as mybir
from concourse.masks import make_identity

K, T, S, N = 512, 2048, 512, 512
FLOPS = 2 * K * N * S

F32 = mybir.dt.float32
BF16 = mybir.dt.bfloat16
I32 = mybir.dt.int32
U32 = mybir.dt.uint32
U16 = mybir.dt.uint16
U8 = mybir.dt.uint8
FP8X4 = mybir.dt.float8_e4m3fn_x4
ALU = mybir.AluOpType
ACT = mybir.ActivationFunctionType

P = 128
PACK = 4
HALF = 256
CHUNKS = ((0, 256), (256, 384), (384, 512))
GROUPS = (((0, 1), (1, 2), (2, 4)), ((0, 4),), ((0, 3), (3, 4)))
TENSOR_CHUNKS = 1


def tile_picked_lamrank_none_po_kernel(tc, x_words, x_scales, w1, dg1, dg2, offs, p1, p2, out_0, out_1, out_2):
    nc = tc.nc
    with ExitStack() as ctx:
        keep = ctx.enter_context(tc.tile_pool(name="keep", bufs=1))
        psum = ctx.enter_context(tc.psum_pool(name="psum", bufs=1))

        offs_sb = keep.tile([P, S // 16], U16, name="offs_sb")
        lists = [keep.tile([P, S // 16], U16, name=f"list{i}") for i in range(2)]
        xw = keep.tile([P, T], U32, name="xw")
        xs_rows = keep.tile([P, T // 4], I32, name="xs_rows")
        xs = keep.tile([P, T // 4], I32, name="xs")
        w_raw = keep.tile([P, PACK * N], F32, name="w_raw", tag="stage")

        nc.vector.memset(xs[:], 0)
        for q in range(4):
            queue = nc.sync if q % 2 == 0 else nc.scalar
            queue.dma_start(xs_rows[32 * q : 32 * q + 4, :], x_scales[0, 4 * q : 4 * q + 4, :].bitcast(I32))
        nc.sync.dma_start(offs_sb[:], offs)
        nc.sync.dma_start(w_raw[:], w1.rearrange("(p j) c -> p (j c)", j=PACK))
        nc.sync.dma_start(xw[:].bitcast(I32), x_words[0].rearrange("p n t -> p (n t)").bitcast(I32))
        nc.sync.dma_start(lists[0][:], p1)
        nc.sync.dma_start(lists[1][:], p2)
        warm = keep.tile([P, 2], F32, name="warm")
        nc.vector.memset(warm[:, 0:1], 0.0)
        nc.scalar.activation(warm[:, 1:2], warm[:, 0:1], ACT.Sigmoid)

        for q in range(4):
            nc.vector.tensor_copy(xs[32 * q : 32 * q + 4, :], xs_rows[32 * q : 32 * q + 4, :])
        ident = keep.tile([P, P], F32, name="ident")
        make_identity(nc, ident[:])
        xs_g = keep.tile([P, S], U8, name="xs_g", align_bytes=64)
        nc.vector.tensor_copy(xs_g[:], xs[:].bitcast(U8).indirect(offs_sb[:]))

        w_src = w_raw[:].rearrange("p (j m t) -> p m t j", j=PACK, t=PACK)
        w_codes, w_scales = [], []
        for pair, copy in enumerate((nc.vector.tensor_copy, nc.scalar.copy)):
            w_bf = keep.tile([P, 2, P, PACK], BF16, name=f"w_bf{pair}", tag=f"w_bf{pair}", align_bytes=64)
            copy(w_bf[:].rearrange("p t m j -> p m t j"), w_src[:, :, 2 * pair : 2 * pair + 2, :])
            codes = keep.tile([P, 2 * P], U32, name=f"w_codes{pair}", align_bytes=64)
            scales = keep.tile([P, 2 * P], U8, name=f"w_scales{pair}", align_bytes=64)
            nc.vector.quantize_mx(codes[:].bitcast(FP8X4), scales[:], w_bf[:].rearrange("p t m j -> p (t m j)"))
            w_codes.append(codes)
            w_scales.append(scales)

        xw_g = keep.tile([P, S], U32, name="xw_g", tag="w_bf0", align_bytes=64)
        for h in range(2):
            nc.vector.tensor_copy(xw_g[:, HALF * h : HALF * h + HALF], xw[:].indirect(offs_sb[:, 16 * h : 16 * h + 16]))

        gain_all = keep.tile([P, 2 * PACK * S], F32, name="gain_all", tag="stage")
        gains = []
        for c0, c1 in CHUNKS:
            g = gain_all[:, 2 * PACK * c0 : 2 * PACK * c1].rearrange("p (i t n) -> p i t n", t=PACK, i=2)
            for i, dg in enumerate((dg1, dg2)):
                nc.sync.dma_start(g[:, i, :, :], dg.rearrange("(p t) s -> p t s", t=PACK)[:, :, c0:c1])
            gains.append(g)

        win = [keep.tile([P, S], F32, name=f"win{t}") for t in range(PACK)]
        banks = [[psum.tile([P, HALF], F32, name=f"bank{t}_{h}", tag=f"bank{t}_{h}") for h in range(2)] for t in range(PACK)]
        plain = [[keep.tile([P, HALF], F32, name=f"plain{t}_{h}") for h in range(2)] for t in range(PACK)]
        for t in range(PACK):
            for h in range(2):
                cols = slice(HALF * h, HALF * h + HALF)
                nc.tensor.matmul_mx(
                    banks[t][h][:],
                    lhsT=w_codes[t // 2][:, P * (t % 2) : P * (t % 2) + P].bitcast(FP8X4),
                    lhsT_scale=w_scales[t // 2][:, P * (t % 2) : P * (t % 2) + P],
                    rhs=xw_g[:, cols].bitcast(FP8X4),
                    rhs_scale=xs_g[:, cols],
                    start=True,
                    stop=True,
                )
                if (t, h) == (0, 1):
                    nc.vector.tensor_copy(win[t][:, cols], banks[t][h][:])
                else:
                    nc.scalar.copy(win[t][:, cols], banks[t][h][:])
                if h == 0:
                    nc.scalar.copy(plain[t][0][:], banks[t][0][:])

        o_scales = keep.tile([P, S], U8, name="o_scales", align_bytes=64)
        out_rows = out_0.rearrange("(p t) s -> p t s", t=PACK)
        words_hbm = out_1[0].rearrange("p n t -> p (n t)").bitcast(I32)
        res = [keep.tile([P, PACK, c1 - c0], F32, name=f"res{c}") for c, (c0, c1) in enumerate(CHUNKS)]
        groups = [(c, t0, t1) for c in range(len(CHUNKS)) for t0, t1 in GROUPS[c]]
        picked, sig, prod, rounded = {}, {}, {}, {}

        def gather(g, t, i):
            c, t0, t1 = groups[g]
            c0, c1 = CHUNKS[c]
            h = c0 // HALF
            if (t, i) == (t0, 0):
                picked[g] = keep.tile([P, 2, t1 - t0, c1 - c0], F32, name=f"picked{g}", tag=f"sig{g - 2}" if g >= 3 else f"picked{g}")
            window = win[t][:].indirect(lists[i][:, c0 // 16 : c1 // 16])
            own = plain[t][h][:, c0 - HALF * h : c1 - HALF * h]
            nc.vector.tensor_tensor(picked[g][:, i, t - t0, :], window, own, ALU.subtract)

        def sigmoid(g):
            c, t0, t1 = groups[g]
            c0, c1 = CHUNKS[c]
            h = c0 // HALF
            diff = picked[g]
            sig[g] = keep.tile([P, 2, t1 - t0, c1 - c0], F32, name=f"sig{g}", tag=f"sig{g}")
            nc.scalar.activation(sig[g][:], diff[:], ACT.Sigmoid)
            if c == 0:
                for t in range(t0, t1):
                    nc.scalar.copy(plain[t][1][:], banks[t][1][:])

        def weigh(eng, g):
            c, t0, t1 = groups[g]
            c0, c1 = CHUNKS[c]
            prod[g] = keep.tile([P, 2, t1 - t0, c1 - c0], F32, name=f"prod{g}")
            eng.tensor_tensor(prod[g][:], sig[g][:], gains[c][:, :, t0:t1, :], ALU.mult)

        turned = {}

        def weave(copy, dst, src):
            copy(dst.rearrange("p (a i) t -> p a t i", i=4), src.rearrange("p t (a i) -> p a t i", i=4))

        def total(eng, g):
            c, t0, t1 = groups[g]
            c0, c1 = CHUNKS[c]
            on_tensor = c < TENSOR_CHUNKS
            if on_tensor:
                for b in range(c0 // P, c1 // P):
                    if t0 == 0:
                        turned[b] = psum.tile([P, PACK, P], F32, name=f"turned{b}", tag=f"bank{b}_0")
                    for t in range(t0, t1):
                        for i in range(2):
                            block = prod[g][:, i, t - t0, P * b - c0 : P * b - c0 + P]
                            nc.tensor.matmul(turned[b][:, t, :], block, ident[:], start=i == 0, stop=i == 1, is_transpose=True)
            else:
                eng.tensor_tensor(res[c][:, t0:t1, :], prod[g][:, 0, :, :], prod[g][:, 1, :, :], ALU.add)
            if t1 < PACK:
                return
            rounded[c] = keep.tile([P, c1 - c0, PACK], BF16, name=f"rounded{c}", align_bytes=64)
            if on_tensor:
                for b in range(c0 // P, c1 // P):
                    cols = slice(P * b - c0, P * b - c0 + P)
                    staged = keep.tile([P, PACK, P], F32, name=f"staged{b}")
                    nc.scalar.copy(staged[:], turned[b][:])
                    back = psum.tile([P, PACK, P], F32, name=f"back{b}", tag=f"bank{b}_1")
                    for t in range(PACK):
                        nc.tensor.transpose(back[:, t, :], staged[:, t, :], ident[:])
                    nc.scalar.copy(res[c][:, :, cols], back[:])
                    weave(nc.scalar.copy, rounded[c][:, cols, :], back[:])
            else:
                mid = (c1 - c0) // 2
                weave(nc.scalar.copy, rounded[c][:, 0:mid, :], res[c][:, :, 0:mid])
                weave(nc.vector.tensor_copy, rounded[c][:, mid:, :], res[c][:, :, mid:])
            nc.sync.dma_start(out_rows[:, :, c0:c1], res[c][:])

        def quantise_chunk(c):
            c0, c1 = CHUNKS[c]
            codes = keep.tile([P, c1 - c0], U32, name=f"codes{c}", align_bytes=64)
            nc.vector.quantize_mx(codes[:].bitcast(FP8X4), o_scales[:, c0:c1], rounded[c][:].rearrange("p n t -> p (n t)"))
            nc.sync.dma_start(words_hbm[:, c0:c1], codes[:].bitcast(I32))

        for g in range(len(groups) + 1):
            steps = [(t, i) for t in range(groups[g][1], groups[g][2]) for i in range(2)] if g < len(groups) else []
            for k, (t, i) in enumerate(steps):
                gather(g, t, i)
                if g >= 1 and k == 0:
                    weigh(nc.vector, g - 1)
                if g >= 1 and k == 1:
                    total(nc.vector, g - 1)
            if steps:
                sigmoid(g)
            else:
                weigh(nc.vector, g - 1)
                total(nc.vector, g - 1)
        for c in range(len(CHUNKS)):
            quantise_chunk(c)
        for q in range(4):
            queue = nc.sync if q % 2 == 0 else nc.scalar
            queue.dma_start(out_2[0, 4 * q : 4 * q + 4, :].bitcast(I32), o_scales[32 * q : 32 * q + 4, :].bitcast(I32))
